import numpy as np
import ml_dtypes


def mxq(x, axis, fmt="e4m3"):
    dtype, down = {"e4m3": (ml_dtypes.float8_e4m3fn, 7), "e5m2": (ml_dtypes.float8_e5m2, 14)}[fmt]
    v = np.moveaxis(np.asarray(x, np.float32).astype(ml_dtypes.bfloat16).astype(np.float64), axis, -1)
    blocks = v.reshape(v.shape[:-1] + (-1, 32))
    amax = np.abs(blocks).max(-1, keepdims=True)
    byte = np.maximum(np.where(amax > 0, np.frexp(amax)[1] - 1 + 127, 0) - down, 1)
    scale = np.exp2(byte - 127.0)
    codes = (blocks / scale).astype(np.float32).astype(dtype).astype(np.float64)
    return np.moveaxis((codes * scale).reshape(v.shape), -1, axis)


WIDE = False


def mx_kscale(k):
    if not WIDE:
        return np.ones(k)
    levels = np.array([10, -10, 5, -5, 0])
    if k % 512:
        return np.exp2(np.random.permutation(np.resize(levels, k // 32))).repeat(32)
    a = np.empty((k // 512, 16))
    for p in range(k // 512):
        a[p, :8] = np.random.permutation(np.resize(levels, 8))
        for g in range(8):
            far = levels[np.abs(levels - a[p, g]) >= 10]
            a[p, g + 8] = far[np.random.randint(len(far))]
    return np.exp2(a.ravel()).repeat(32)


def f64(x):
    return np.asarray(x).astype(np.float64)


def striped(idx):
    return np.tile(np.asarray(idx).reshape(-1, 16).T, (8, 1)).astype(np.uint16)


def unstriped(offs):
    return offs[:16].T.reshape(-1).astype(np.int64)


E2M1 = np.array([0.0, 0.5, 1.0, 1.5, 2.0, 3.0, 4.0, 6.0, -0.0, -0.5, -1.0, -1.5, -2.0, -3.0, -4.0, -6.0])


def pack_weight(w, fmt):
    k, n = w.shape
    w = f64(np.asarray(w, np.float32).astype(ml_dtypes.bfloat16)).reshape(k // 32, 32, n)
    amax = np.abs(w).max(1)
    if fmt == "e4m3":
        byte = np.frexp(amax)[1] - 1 + 127 - 7
    else:
        mant, ex = np.frexp(amax / 6.0)
        byte = np.where(mant > 0.5, ex, ex - 1) + 127
    byte = np.clip(np.where(amax > 0, byte, 1), 1, 254)
    scaled = (w * np.exp2(127.0 - byte)[:, None, :]).reshape(k, n).astype(np.float32)
    by_word = np.ascontiguousarray(scaled.reshape(k // 512, 128, 4, n).transpose(0, 1, 3, 2))
    if fmt == "e4m3":
        words = by_word.astype(ml_dtypes.float8_e4m3fn).view(np.uint8)
    else:
        c = by_word.astype(ml_dtypes.float4_e2m1fn).view(np.uint8) & 0xF
        words = (c[..., 0::2] | (c[..., 1::2] << 4)).reshape(k // 512, 128, 2 * n)
    return np.ascontiguousarray(words), np.ascontiguousarray(byte.astype(np.uint8).reshape(k // 512, 16, n))


def unpack_weight(words, scales, fmt):
    g, _, n = scales.shape
    words = np.ascontiguousarray(words).reshape(g, 128, n, -1)
    if fmt == "e4m3":
        vals = words.view(ml_dtypes.float8_e4m3fn).astype(np.float64)
    else:
        nib = np.empty((g, 128, n, 4), np.uint8)
        nib[..., 0::2] = words & 0xF
        nib[..., 1::2] = words >> 4
        vals = E2M1[nib]
    vals = vals * np.repeat(np.exp2(scales.astype(np.float64) - 127.0), 8, axis=1)[..., None]
    return vals.transpose(0, 1, 3, 2).reshape(g * 512, n)


D, T, I, Q, E = 512, 2048, 512, 128, 512


def setup_inputs():
    n = np.random.standard_normal
    idx = np.random.permutation(T)[:I]
    fd = mx_kscale(D)
    fi = mx_kscale(I)
    ti = np.ones(T)
    ti[idx] = fi
    keysp = pack_weight(n((D, T)) / fd[:, None], "e4m3")
    return {
        "query": (n((D, Q)) * 0.5 / np.sqrt(D) * fd[:, None]).astype(np.float32),
        "query2": (n((D, Q)) * 0.5 / np.sqrt(D) * fd[:, None]).astype(np.float32),
        "keys_words": keysp[0],
        "keys_scales": keysp[1],
        "share": np.tile(np.random.uniform(0.0, 1.0, T), (128, 1)).astype(np.float32),
        "size": (np.random.uniform(0.5, 2.0, (1, I)) * fi).astype(np.float32),
        "vals": (n((E, T)) / ti).astype(np.float32),
        "offs": striped(idx),
    }


def reference(query, query2, keys_words, keys_scales, share, size, vals, offs):
    idx = unstriped(offs)
    keysu = unpack_weight(keys_words, keys_scales, "e4m3")
    queryq = mxq(f64(query), 0, "e4m3")
    keysidxg = keysu[:, idx]
    a = queryq.T @ keysidxg
    query2q = mxq(f64(query2), 0, "e4m3")
    b = query2q.T @ keysidxg
    s = b + (a - b) * f64(share)[:1][:, idx]
    p = np.exp(s - np.max(s, axis=1, keepdims=True))
    w = p * f64(size) / np.sum(p, axis=1, keepdims=True)
    wt = w.T
    vt = f64(vals)[:, idx].T
    wtq = mxq(wt, 0, "e4m3")
    vtq = mxq(vt, 0, "e4m3")
    o = wtq.T @ vtq
    return o

@@ -1,0 +1,176 @@
+from contextlib import ExitStack
+
+import concourse.mybir as mybir
+from concourse.masks import make_identity
+
+D, T, I, Q, E = 512, 2048, 512, 128, 512
+FLOPS = 3 * 2 * 512 * 128 * 512
+
+F32 = mybir.dt.float32
+BF16 = mybir.dt.bfloat16
+I32 = mybir.dt.int32
+U32 = mybir.dt.uint32
+U16 = mybir.dt.uint16
+U8 = mybir.dt.uint8
+FP8X4 = mybir.dt.float8_e4m3fn_x4
+ALU = mybir.AluOpType
+ACT = mybir.ActivationFunctionType
+AX = mybir.AxisListType
+
+P = 128
+PACK = 4
+LAST = P - 1
+
+
+def tile_attend_slotmixture_kernel(tc, query, query2, keys_words, keys_scales, share, size, vals, offs, out):
+    nc = tc.nc
+    with ExitStack() as ctx:
+        sb = ctx.enter_context(tc.tile_pool(name="sb", bufs=1))
+        ps = ctx.enter_context(tc.psum_pool(name="ps", bufs=1))
+
+        offsets = sb.tile([P, I // 16], U16, name="offsets")
+        nc.sync.dma_start(offsets[:], offs)
+
+        scale_pool = sb.tile([P, T // 4], I32, name="scale_pool", align_bytes=64)
+        nc.sync.dma_start(scale_pool[48:64, :], keys_scales[0].bitcast(I32))
+        nc.gpsimd.memset(scale_pool[0:48, :], 0)
+        nc.gpsimd.memset(scale_pool[64:P, :], 0)
+        share_pool = sb.tile([P, T], F32, name="share_pool", tag="pool_a", align_bytes=64)
+        nc.sync.dma_start(share_pool[LAST:P, :], share[0:1, :])
+        warm = sb.tile([P, 2, 8], F32, name="warm")
+        nc.vector.memset(warm[:, 0, :], 0.0)
+        nc.vector.memset(share_pool[0:LAST, :], 0.0)
+        size_cols = sb.tile([P, PACK], F32, name="size_cols")
+        nc.scalar.dma_start(size_cols[:], size.rearrange("o (p t) -> (o p) t", t=PACK))
+        key_pool = sb.tile([P, T], I32, name="key_pool", tag="pool_b", align_bytes=64)
+        nc.sync.dma_start(key_pool[:], keys_words[0].rearrange("p n t -> p (n t)").bitcast(I32))
+
+        q_raw = sb.tile([P, 2, PACK, Q], F32, name="q_raw", tag="pool_c", align_bytes=64)
+        for n, src in enumerate((query, query2)):
+            nc.sync.dma_start(q_raw[:, n], src.rearrange("(p j) w -> p j w", j=PACK))
+        val_pool = []
+
+        def load_values(c, tag):
+            rows = sb.tile([P, T], F32, name="val_pool%d" % c, tag=tag, align_bytes=64)
+            nc.sync.dma_start(rows[:], vals[c * P : (c + 1) * P, :])
+            val_pool.append(rows)
+
+        load_values(0, "pool_d")
+
+        ident = sb.tile([P, P], F32, name="ident")
+        make_identity(nc, ident[:])
+
+        nc.scalar.activation(warm[:, 1, 0:1], warm[:, 0, 0:1], ACT.Exp)
+
+        scale_g = sb.tile([P, I], U8, name="scale_g", align_bytes=64)
+        nc.vector.tensor_copy(scale_g[:], scale_pool[:].bitcast(U8).indirect(offsets[:]))
+        key_scales = sb.tile([P, I], U8, name="key_scales", align_bytes=64)
+        nc.gpsimd.memset(key_scales[:].bitcast(I32), 0)
+        for quad in range(4):
+            nc.scalar.dma_start(key_scales[32 * quad : 32 * quad + 4, :].bitcast(I32), scale_g[48 + 4 * quad : 52 + 4 * quad, :].bitcast(I32))
+        share_g = sb.tile([P, I], F32, name="share_g", align_bytes=64)
+        nc.vector.tensor_copy(share_g[:], share_pool[:].indirect(offsets[:]))
+        load_values(1, "pool_a")
+        key_words = sb.tile([P, I], U32, name="key_words", align_bytes=64)
+        nc.vector.tensor_copy(key_words[:], key_pool[:].bitcast(U32).indirect(offsets[:]))
+        load_values(2, "pool_b")
+
+        share_t = ps.tile([P, 4, P], F32, name="share_t", tag="turn")
+        for j in range(4):
+            nc.tensor.transpose(share_t[:, j, :], share_g[:, j * P : (j + 1) * P], ident[:])
+        mix = sb.tile([P, 2, 8], F32, name="mix")
+        nc.scalar.copy(mix[:, 0, 0:4], share_t[:, :, LAST])
+        nc.scalar.activation(mix[:, 1, 0:4], share_t[:, :, LAST], ACT.Identity, bias=1.0, scale=-1.0)
+
+        size_rows = ps.tile([P, PACK, P], F32, name="size_rows")
+        for t in range(PACK):
+            nc.tensor.transpose(size_rows[:, t, :], size_cols[:, t : t + 1].to_broadcast([P, P]), ident[:])
+
+        q_grouped = sb.tile([P, 2, Q, PACK], BF16, name="q_grouped", align_bytes=64)
+        for n in range(2):
+            nc.scalar.copy(q_grouped[:, n], q_raw[:, n].rearrange("p j w -> p w j"))
+        load_values(3, "pool_c")
+        q_codes = sb.tile([P, 2 * Q], U32, name="q_codes", align_bytes=64)
+        q_scales = sb.tile([P, 2 * Q], U8, name="q_scales", align_bytes=64)
+        nc.vector.quantize_mx(q_codes[:].bitcast(FP8X4), q_scales[:], q_grouped[:].rearrange("p n w j -> p (n w j)"))
+
+        parts = []
+        for h in range(2):
+            bank = ps.tile([P, 2, 2, Q], F32, name="score%d" % h, tag="acc", bufs=2)
+            for jj in range(2):
+                j = 2 * h + jj
+                cols = slice(j * P, (j + 1) * P)
+                nc.tensor.matmul_mx(
+                    bank[:, jj].rearrange("p n q -> p (n q)"),
+                    lhsT=key_words[:, cols].bitcast(FP8X4),
+                    lhsT_scale=key_scales[:, cols],
+                    rhs=q_codes[:].bitcast(FP8X4),
+                    rhs_scale=q_scales[:],
+                    start=True,
+                    stop=True,
+                )
+            for jj in range(2):
+                j = 2 * h + jj
+                part = sb.tile([P, 2, Q], F32, name="part%d" % j)
+                for n in range(2):
+                    nc.scalar.activation(part[:, n, :], bank[:, jj, n, :], ACT.Copy, scale=mix[:, n, j : j + 1])
+                parts.append(part)
+        mixed = ps.tile([P, I], F32, name="mixed")
+        for j in range(4):
+            for n in range(2):
+                nc.tensor.matmul(mixed[:, j * P : (j + 1) * P], parts[j][:, n, :], ident[:], start=(n == 0), stop=(n == 1), is_transpose=True)
+
+        neg_max = sb.tile([P, 1], F32, name="neg_max")
+        nc.vector.tensor_reduce(neg_max[:], mixed[:], AX.X, ALU.max, negate=True)
+        probs = sb.tile([P, I], F32, name="probs")
+        total = sb.tile([P, 1], F32, name="total")
+        nc.scalar.activation(probs[:], mixed[:], ACT.Exp, bias=neg_max[:], scale=1.0, accum_out=total[:])
+        inv_total = sb.tile([P, 1], F32, name="inv_total")
+        nc.vector.reciprocal(inv_total[:], total[:])
+        weights = sb.tile([P, I], BF16, name="weights", align_bytes=64)
+        nc.vector.scalar_tensor_tensor(
+            weights[:].rearrange("q (p t) -> q p t", t=PACK),
+            probs[:].rearrange("q (p t) -> q p t", t=PACK),
+            inv_total[:],
+            size_rows[:].rearrange("q t p -> q p t"),
+            ALU.mult,
+            ALU.mult,
+        )
+
+
+        def turn_and_quantize(name, tiles, tag, bufs):
+            n = len(tiles)
+            turned = ps.tile([P, n, 2, P], F32, name=name + "_turned", tag=tag, bufs=bufs)
+            for a, tile in enumerate(tiles):
+                words = tile[:].bitcast(F32)
+                for u in range(2):
+                    nc.tensor.transpose(turned[:, a, u, :], words[:, u : I // 2 : 2], ident[:])
+            grouped = sb.tile([P, n, P, 2], F32, name=name + "_grouped", align_bytes=64)
+            nc.scalar.copy(grouped[:], turned[:].rearrange("p a u x -> p a x u"))
+            codes = sb.tile([P, n * P], U32, name=name + "_codes", align_bytes=64)
+            scales = sb.tile([P, n * P], U8, name=name + "_scales", align_bytes=64)
+            nc.vector.quantize_mx(codes[:].bitcast(FP8X4), scales[:], grouped[:].rearrange("p a x u -> p (a x u)").bitcast(BF16))
+            return codes, scales
+
+        w_codes, w_scales = turn_and_quantize("w", [weights], "turn", 1)
+
+        for first, count in ((0, 2), (2, 1), (3, 1)):
+            gathered = []
+            for c in range(first, first + count):
+                g = sb.tile([P, I], BF16, name="val_g%d" % c, align_bytes=64)
+                nc.vector.tensor_copy(g[:], val_pool[c][:].indirect(offsets[:]))
+                gathered.append(g)
+            v_codes, v_scales = turn_and_quantize("v%d" % first, gathered, "vturn", 2)
+            acc = ps.tile([P, count * P], F32, name="acc%d" % first, tag="acc", bufs=2)
+            nc.tensor.matmul_mx(
+                acc[:],
+                lhsT=w_codes[:].bitcast(FP8X4),
+                lhsT_scale=w_scales[:],
+                rhs=v_codes[:].bitcast(FP8X4),
+                rhs_scale=v_scales[:],
+                start=True,
+                stop=True,
+            )
+            result = sb.tile([P, count * P], F32, name="result%d" % first)
+            nc.scalar.copy(result[:], acc[:])
+            nc.sync.dma_start(out[:, first * P : (first + count) * P], result[:])

@@ -20,6 +20,7 @@ AX = mybir.AxisListType
 P = 128
 PACK = 4
 LAST = P - 1
+SPLIT = 1024
 
 
 def tile_attend_slotmixture_kernel(tc, query, query2, keys_words, keys_scales, share, size, vals, offs, out):
@@ -31,23 +32,22 @@ def tile_attend_slotmixture_kernel(tc, query, query2, keys_words, keys_scales, s
         offsets = sb.tile([P, I // 16], U16, name="offsets")
         nc.sync.dma_start(offsets[:], offs)
 
-        scale_pool = sb.tile([P, T // 4], I32, name="scale_pool", align_bytes=64)
-        nc.sync.dma_start(scale_pool[48:64, :], keys_scales[0].bitcast(I32))
-        nc.gpsimd.memset(scale_pool[0:48, :], 0)
-        nc.gpsimd.memset(scale_pool[64:P, :], 0)
-        share_pool = sb.tile([P, T], F32, name="share_pool", tag="pool_a", align_bytes=64)
-        nc.sync.dma_start(share_pool[LAST:P, :], share[0:1, :])
+        scale_pool = sb.tile([P, T // 4], I32, name="scale_pool", tag="pool_e", align_bytes=64)
+        nc.vector.memset(scale_pool[:], 0)
+        for quad in range(4):
+            nc.scalar.dma_start(scale_pool[32 * quad : 32 * quad + 4, :], keys_scales[0, 4 * quad : 4 * quad + 4, :].bitcast(I32))
         warm = sb.tile([P, 2, 8], F32, name="warm")
         nc.vector.memset(warm[:, 0, :], 0.0)
-        nc.vector.memset(share_pool[0:LAST, :], 0.0)
-        size_cols = sb.tile([P, PACK], F32, name="size_cols")
-        nc.scalar.dma_start(size_cols[:], size.rearrange("o (p t) -> (o p) t", t=PACK))
-        key_pool = sb.tile([P, T], I32, name="key_pool", tag="pool_b", align_bytes=64)
-        nc.sync.dma_start(key_pool[:], keys_words[0].rearrange("p n t -> p (n t)").bitcast(I32))
-
+        share_pool = sb.tile([P, T], F32, name="share_pool", tag="pool_a", align_bytes=64)
+        nc.sync.dma_start(share_pool[LAST:P, :], share[0:1, :])
+        nc.gpsimd.memset(share_pool[0:LAST, 0:SPLIT], 0.0)
+        nc.vector.memset(share_pool[0:LAST, SPLIT:T], 0.0)
         q_raw = sb.tile([P, 2, PACK, Q], F32, name="q_raw", tag="pool_c", align_bytes=64)
         for n, src in enumerate((query, query2)):
             nc.sync.dma_start(q_raw[:, n], src.rearrange("(p j) w -> p j w", j=PACK))
+        key_pool = sb.tile([P, T], I32, name="key_pool", align_bytes=64)
+        nc.sync.dma_start(key_pool[:], keys_words[0].rearrange("p n t -> p (n t)").bitcast(I32))
+
         val_pool = []
 
         def load_values(c, tag):
@@ -55,25 +55,20 @@ def tile_attend_slotmixture_kernel(tc, query, query2, keys_words, keys_scales, s
             nc.sync.dma_start(rows[:], vals[c * P : (c + 1) * P, :])
             val_pool.append(rows)
 
-        load_values(0, "pool_d")
-
         ident = sb.tile([P, P], F32, name="ident")
         make_identity(nc, ident[:])
+        size_cols = sb.tile([P, PACK], F32, name="size_cols")
+        nc.gpsimd.dma_start(size_cols[:], size.rearrange("o (p t) -> (o p) t", t=PACK))
 
         nc.scalar.activation(warm[:, 1, 0:1], warm[:, 0, 0:1], ACT.Exp)
 
-        scale_g = sb.tile([P, I], U8, name="scale_g", align_bytes=64)
-        nc.vector.tensor_copy(scale_g[:], scale_pool[:].bitcast(U8).indirect(offsets[:]))
-        key_scales = sb.tile([P, I], U8, name="key_scales", align_bytes=64)
-        nc.gpsimd.memset(key_scales[:].bitcast(I32), 0)
-        for quad in range(4):
-            nc.scalar.dma_start(key_scales[32 * quad : 32 * quad + 4, :].bitcast(I32), scale_g[48 + 4 * quad : 52 + 4 * quad, :].bitcast(I32))
         share_g = sb.tile([P, I], F32, name="share_g", align_bytes=64)
         nc.vector.tensor_copy(share_g[:], share_pool[:].indirect(offsets[:]))
-        load_values(1, "pool_a")
+        load_values(0, "pool_a")
+        key_scales = sb.tile([P, I], U8, name="key_scales", align_bytes=64)
+        nc.vector.tensor_copy(key_scales[:], scale_pool[:].bitcast(U8).indirect(offsets[:]))
         key_words = sb.tile([P, I], U32, name="key_words", align_bytes=64)
         nc.vector.tensor_copy(key_words[:], key_pool[:].bitcast(U32).indirect(offsets[:]))
-        load_values(2, "pool_b")
 
         share_t = ps.tile([P, 4, P], F32, name="share_t", tag="turn")
         for j in range(4):
@@ -82,14 +77,11 @@ def tile_attend_slotmixture_kernel(tc, query, query2, keys_words, keys_scales, s
         nc.scalar.copy(mix[:, 0, 0:4], share_t[:, :, LAST])
         nc.scalar.activation(mix[:, 1, 0:4], share_t[:, :, LAST], ACT.Identity, bias=1.0, scale=-1.0)
 
-        size_rows = ps.tile([P, PACK, P], F32, name="size_rows")
-        for t in range(PACK):
-            nc.tensor.transpose(size_rows[:, t, :], size_cols[:, t : t + 1].to_broadcast([P, P]), ident[:])
-
         q_grouped = sb.tile([P, 2, Q, PACK], BF16, name="q_grouped", align_bytes=64)
         for n in range(2):
             nc.scalar.copy(q_grouped[:, n], q_raw[:, n].rearrange("p j w -> p w j"))
-        load_values(3, "pool_c")
+        load_values(1, "pool_c")
+        load_values(2, "pool_e")
         q_codes = sb.tile([P, 2 * Q], U32, name="q_codes", align_bytes=64)
         q_scales = sb.tile([P, 2 * Q], U8, name="q_scales", align_bytes=64)
         nc.vector.quantize_mx(q_codes[:].bitcast(FP8X4), q_scales[:], q_grouped[:].rearrange("p n w j -> p (n w j)"))
@@ -120,12 +112,25 @@ def tile_attend_slotmixture_kernel(tc, query, query2, keys_words, keys_scales, s
             for n in range(2):
                 nc.tensor.matmul(mixed[:, j * P : (j + 1) * P], parts[j][:, n, :], ident[:], start=(n == 0), stop=(n == 1), is_transpose=True)
 
-        neg_max = sb.tile([P, 1], F32, name="neg_max")
+        size_rows = ps.tile([P, PACK, P], F32, name="size_rows", tag="acc", bufs=2)
+        for t in range(PACK):
+            nc.tensor.transpose(size_rows[:, t, :], size_cols[:, t : t + 1].to_broadcast([P, P]), ident[:])
+
+        def gather_values(c):
+            g = sb.tile([P, I], BF16, name="val_g%d" % c, align_bytes=64)
+            nc.vector.tensor_copy(g[:], val_pool[c][:].indirect(offsets[:]))
+            return g
+
+        g0 = gather_values(0)
+        load_values(3, "pool_a")
+        g1 = gather_values(1)
+        neg_max = sb.tile([P, 1], F32, name="neg_max", tag="pool_c", align_bytes=64)
         nc.vector.tensor_reduce(neg_max[:], mixed[:], AX.X, ALU.max, negate=True)
         probs = sb.tile([P, I], F32, name="probs")
         total = sb.tile([P, 1], F32, name="total")
         nc.scalar.activation(probs[:], mixed[:], ACT.Exp, bias=neg_max[:], scale=1.0, accum_out=total[:])
-        inv_total = sb.tile([P, 1], F32, name="inv_total")
+        g2 = gather_values(2)
+        inv_total = sb.tile([P, 1], F32, name="inv_total", tag="pool_e", align_bytes=64)
         nc.vector.reciprocal(inv_total[:], total[:])
         weights = sb.tile([P, I], BF16, name="weights", align_bytes=64)
         nc.vector.scalar_tensor_tensor(
@@ -137,40 +142,58 @@ def tile_attend_slotmixture_kernel(tc, query, query2, keys_words, keys_scales, s
             ALU.mult,
         )
 
-
-        def turn_and_quantize(name, tiles, tag, bufs):
-            n = len(tiles)
-            turned = ps.tile([P, n, 2, P], F32, name=name + "_turned", tag=tag, bufs=bufs)
+        def turn(name, tiles, grouped):
+            turned = ps.tile([P, len(tiles), 2, P], F32, name=name, tag="vturn", bufs=2)
             for a, tile in enumerate(tiles):
                 words = tile[:].bitcast(F32)
                 for u in range(2):
                     nc.tensor.transpose(turned[:, a, u, :], words[:, u : I // 2 : 2], ident[:])
-            grouped = sb.tile([P, n, P, 2], F32, name=name + "_grouped", align_bytes=64)
-            nc.scalar.copy(grouped[:], turned[:].rearrange("p a u x -> p a x u"))
-            codes = sb.tile([P, n * P], U32, name=name + "_codes", align_bytes=64)
-            scales = sb.tile([P, n * P], U8, name=name + "_scales", align_bytes=64)
-            nc.vector.quantize_mx(codes[:].bitcast(FP8X4), scales[:], grouped[:].rearrange("p a x u -> p (a x u)").bitcast(BF16))
-            return codes, scales
+            nc.scalar.copy(grouped.rearrange("p (a x u) -> p a x u", x=P, u=2), turned[:].rearrange("p a u x -> p a x u"))
 
-        w_codes, w_scales = turn_and_quantize("w", [weights], "turn", 1)
-
-        for first, count in ((0, 2), (2, 1), (3, 1)):
-            gathered = []
-            for c in range(first, first + count):
-                g = sb.tile([P, I], BF16, name="val_g%d" % c, align_bytes=64)
-                nc.vector.tensor_copy(g[:], val_pool[c][:].indirect(offsets[:]))
-                gathered.append(g)
-            v_codes, v_scales = turn_and_quantize("v%d" % first, gathered, "vturn", 2)
+        def multiply(first, count, v_codes, v_scales):
             acc = ps.tile([P, count * P], F32, name="acc%d" % first, tag="acc", bufs=2)
             nc.tensor.matmul_mx(
                 acc[:],
-                lhsT=w_codes[:].bitcast(FP8X4),
-                lhsT_scale=w_scales[:],
-                rhs=v_codes[:].bitcast(FP8X4),
-                rhs_scale=v_scales[:],
+                lhsT=codes[:, 0:P].bitcast(FP8X4),
+                lhsT_scale=scales[:, 0:P],
+                rhs=v_codes.bitcast(FP8X4),
+                rhs_scale=v_scales,
                 start=True,
                 stop=True,
             )
-            result = sb.tile([P, count * P], F32, name="result%d" % first)
-            nc.scalar.copy(result[:], acc[:])
-            nc.sync.dma_start(out[:, first * P : (first + count) * P], result[:])
+            return acc
+
+        g3 = gather_values(3)
+        grouped = sb.tile([P, 8 * P], F32, name="grouped", align_bytes=64)
+        turn("turned01", [g0, g1], grouped[:, 2 * P : 6 * P])
+        turn("turned2", [g2], grouped[:, 6 * P : 8 * P])
+        turn("turnedw", [weights], grouped[:, 0 : 2 * P])
+        last_grouped = sb.tile([P, 2 * P], F32, name="last_grouped", align_bytes=64)
+        turn("turned3", [g3], last_grouped[:])
+
+        codes = sb.tile([P, 4 * P], U32, name="codes", tag="pool_a", align_bytes=64)
+        scales = sb.tile([P, 4 * P], U8, name="scales", align_bytes=64)
+        nc.vector.quantize_mx(codes[:].bitcast(FP8X4), scales[:], grouped[:].bitcast(BF16))
+        last_codes = sb.tile([P, P], U32, name="last_codes", align_bytes=64)
+        last_scales = sb.tile([P, P], U8, name="last_scales", align_bytes=64)
+        nc.vector.quantize_mx(last_codes[:].bitcast(FP8X4), last_scales[:], last_grouped[:].bitcast(BF16))
+
+        result = sb.tile([P, 3 * P], F32, name="result")
+        acc = multiply(0, 2, codes[:, P : 3 * P], scales[:, P : 3 * P])
+        nc.scalar.copy(result[:, 0 : 2 * P], acc[:])
+        acc = multiply(2, 1, codes[:, 3 * P : 4 * P], scales[:, 3 * P : 4 * P])
+        nc.scalar.copy(result[:, 2 * P : 3 * P], acc[:])
+        nc.sync.dma_start(out[:, 0 : 3 * P], result[:])
+        last_acc = ps.tile([P, P], F32, name="last_acc", tag="turn")
+        nc.tensor.matmul_mx(
+            last_acc[:],
+            lhsT=codes[:, 0:P].bitcast(FP8X4),
+            lhsT_scale=scales[:, 0:P],
+            rhs=last_codes[:].bitcast(FP8X4),
+            rhs_scale=last_scales[:],
+            start=True,
+            stop=True,
+        )
+        last_result = sb.tile([P, P], F32, name="last_result")
+        nc.vector.tensor_copy(last_result[:], last_acc[:])
+        nc.scalar.dma_start(out[:, 3 * P : 4 * P], last_result[:])

@@ -20,7 +20,6 @@ AX = mybir.AxisListType
 P = 128
 PACK = 4
 LAST = P - 1
-SPLIT = 1024
 
 
 def tile_attend_slotmixture_kernel(tc, query, query2, keys_words, keys_scales, share, size, vals, offs, out):
@@ -36,16 +35,16 @@ def tile_attend_slotmixture_kernel(tc, query, query2, keys_words, keys_scales, s
         nc.vector.memset(scale_pool[:], 0)
         for quad in range(4):
             nc.scalar.dma_start(scale_pool[32 * quad : 32 * quad + 4, :], keys_scales[0, 4 * quad : 4 * quad + 4, :].bitcast(I32))
-        warm = sb.tile([P, 2, 8], F32, name="warm")
-        nc.vector.memset(warm[:, 0, :], 0.0)
+        size_pad = sb.tile([P, P], F32, name="size_pad")
+        nc.vector.memset(size_pad[0 : P - 4, :], 0.0)
+        nc.scalar.dma_start(size_pad[P - 4 : P, :], size.rearrange("o (j p) -> (o j) p", p=P))
         share_pool = sb.tile([P, T], F32, name="share_pool", tag="pool_a", align_bytes=64)
         nc.sync.dma_start(share_pool[LAST:P, :], share[0:1, :])
-        nc.gpsimd.memset(share_pool[0:LAST, 0:SPLIT], 0.0)
-        nc.vector.memset(share_pool[0:LAST, SPLIT:T], 0.0)
+        nc.vector.memset(share_pool[0:LAST, :], 0.0)
         q_raw = sb.tile([P, 2, PACK, Q], F32, name="q_raw", tag="pool_c", align_bytes=64)
         for n, src in enumerate((query, query2)):
             nc.sync.dma_start(q_raw[:, n], src.rearrange("(p j) w -> p j w", j=PACK))
-        key_pool = sb.tile([P, T], I32, name="key_pool", align_bytes=64)
+        key_pool = sb.tile([P, T], I32, name="key_pool", tag="pool_b", align_bytes=64)
         nc.sync.dma_start(key_pool[:], keys_words[0].rearrange("p n t -> p (n t)").bitcast(I32))
 
         val_pool = []
@@ -55,19 +54,18 @@ def tile_attend_slotmixture_kernel(tc, query, query2, keys_words, keys_scales, s
             nc.sync.dma_start(rows[:], vals[c * P : (c + 1) * P, :])
             val_pool.append(rows)
 
+        load_values(0, "pool_d")
         ident = sb.tile([P, P], F32, name="ident")
         make_identity(nc, ident[:])
-        size_cols = sb.tile([P, PACK], F32, name="size_cols")
-        nc.gpsimd.dma_start(size_cols[:], size.rearrange("o (p t) -> (o p) t", t=PACK))
-
-        nc.scalar.activation(warm[:, 1, 0:1], warm[:, 0, 0:1], ACT.Exp)
+        warm = sb.tile([P, 8], F32, name="warm")
+        nc.scalar.activation(warm[0:64, 0:1], size_pad[0:64, 0:1], ACT.Exp)
 
         share_g = sb.tile([P, I], F32, name="share_g", align_bytes=64)
         nc.vector.tensor_copy(share_g[:], share_pool[:].indirect(offsets[:]))
-        load_values(0, "pool_a")
+        load_values(1, "pool_a")
         key_scales = sb.tile([P, I], U8, name="key_scales", align_bytes=64)
         nc.vector.tensor_copy(key_scales[:], scale_pool[:].bitcast(U8).indirect(offsets[:]))
-        key_words = sb.tile([P, I], U32, name="key_words", align_bytes=64)
+        key_words = sb.tile([P, I], U32, name="key_words", tag="pool_e", align_bytes=64)
         nc.vector.tensor_copy(key_words[:], key_pool[:].bitcast(U32).indirect(offsets[:]))
 
         share_t = ps.tile([P, 4, P], F32, name="share_t", tag="turn")
@@ -77,11 +75,15 @@ def tile_attend_slotmixture_kernel(tc, query, query2, keys_words, keys_scales, s
         nc.scalar.copy(mix[:, 0, 0:4], share_t[:, :, LAST])
         nc.scalar.activation(mix[:, 1, 0:4], share_t[:, :, LAST], ACT.Identity, bias=1.0, scale=-1.0)
 
+        size_t = ps.tile([P, P], F32, name="size_t")
+        nc.tensor.transpose(size_t[:], size_pad[:], ident[:])
+        size_cols = sb.tile([P, 4], F32, name="size_cols")
+        nc.scalar.copy(size_cols[:], size_t[:, P - 4 : P])
+
         q_grouped = sb.tile([P, 2, Q, PACK], BF16, name="q_grouped", align_bytes=64)
         for n in range(2):
             nc.scalar.copy(q_grouped[:, n], q_raw[:, n].rearrange("p j w -> p w j"))
-        load_values(1, "pool_c")
-        load_values(2, "pool_e")
+        load_values(2, "pool_c")
         q_codes = sb.tile([P, 2 * Q], U32, name="q_codes", align_bytes=64)
         q_scales = sb.tile([P, 2 * Q], U8, name="q_scales", align_bytes=64)
         nc.vector.quantize_mx(q_codes[:].bitcast(FP8X4), q_scales[:], q_grouped[:].rearrange("p n w j -> p (n w j)"))
@@ -117,33 +119,33 @@ def tile_attend_slotmixture_kernel(tc, query, query2, keys_words, keys_scales, s
             nc.tensor.transpose(size_rows[:, t, :], size_cols[:, t : t + 1].to_broadcast([P, P]), ident[:])
 
         def gather_values(c):
-            g = sb.tile([P, I], BF16, name="val_g%d" % c, align_bytes=64)
+            g = sb.tile([P, I], BF16, name="val_g%d" % c, tag="pool_b" if c == 0 else "val_g%d" % c, align_bytes=64)
             nc.vector.tensor_copy(g[:], val_pool[c][:].indirect(offsets[:]))
             return g
 
         g0 = gather_values(0)
-        load_values(3, "pool_a")
+        load_values(3, "pool_d")
         g1 = gather_values(1)
-        neg_max = sb.tile([P, 1], F32, name="neg_max", tag="pool_c", align_bytes=64)
+        neg_max = sb.tile([P, 1], F32, name="neg_max", tag="pool_a", align_bytes=64)
         nc.vector.tensor_reduce(neg_max[:], mixed[:], AX.X, ALU.max, negate=True)
         probs = sb.tile([P, I], F32, name="probs")
         total = sb.tile([P, 1], F32, name="total")
         nc.scalar.activation(probs[:], mixed[:], ACT.Exp, bias=neg_max[:], scale=1.0, accum_out=total[:])
         g2 = gather_values(2)
-        inv_total = sb.tile([P, 1], F32, name="inv_total", tag="pool_e", align_bytes=64)
+        inv_total = sb.tile([P, 1], F32, name="inv_total", tag="pool_c", align_bytes=64)
         nc.vector.reciprocal(inv_total[:], total[:])
         weights = sb.tile([P, I], BF16, name="weights", align_bytes=64)
         nc.vector.scalar_tensor_tensor(
-            weights[:].rearrange("q (p t) -> q p t", t=PACK),
-            probs[:].rearrange("q (p t) -> q p t", t=PACK),
+            weights[:],
+            probs[:],
             inv_total[:],
-            size_rows[:].rearrange("q t p -> q p t"),
+            size_rows[:].rearrange("q j p -> q (j p)"),
             ALU.mult,
             ALU.mult,
         )
 
-        def turn(name, tiles, grouped):
-            turned = ps.tile([P, len(tiles), 2, P], F32, name=name, tag="vturn", bufs=2)
+        def turn(name, tiles, grouped, tag):
+            turned = ps.tile([P, len(tiles), 2, P], F32, name=name, tag=tag, bufs=2)
             for a, tile in enumerate(tiles):
                 words = tile[:].bitcast(F32)
                 for u in range(2):
@@ -165,13 +167,13 @@ def tile_attend_slotmixture_kernel(tc, query, query2, keys_words, keys_scales, s
 
         g3 = gather_values(3)
         grouped = sb.tile([P, 8 * P], F32, name="grouped", align_bytes=64)
-        turn("turned01", [g0, g1], grouped[:, 2 * P : 6 * P])
-        turn("turned2", [g2], grouped[:, 6 * P : 8 * P])
-        turn("turnedw", [weights], grouped[:, 0 : 2 * P])
+        turn("turned01", [g0, g1], grouped[:, 2 * P : 6 * P], "acc")
+        turn("turned2", [g2], grouped[:, 6 * P : 8 * P], "vturn")
+        turn("turnedw", [weights], grouped[:, 0 : 2 * P], "vturn")
         last_grouped = sb.tile([P, 2 * P], F32, name="last_grouped", align_bytes=64)
-        turn("turned3", [g3], last_grouped[:])
+        turn("turned3", [g3], last_grouped[:], "vturn")
 
-        codes = sb.tile([P, 4 * P], U32, name="codes", tag="pool_a", align_bytes=64)
+        codes = sb.tile([P, 4 * P], U32, name="codes", tag="pool_d", align_bytes=64)
         scales = sb.tile([P, 4 * P], U8, name="scales", align_bytes=64)
         nc.vector.quantize_mx(codes[:].bitcast(FP8X4), scales[:], grouped[:].bitcast(BF16))
         last_codes = sb.tile([P, P], U32, name="last_codes", align_bytes=64)

@@ -4,7 +4,7 @@ import concourse.mybir as mybir
 from concourse.masks import make_identity
 
 D, T, I, Q, E = 512, 2048, 512, 128, 512
-FLOPS = 3 * 2 * 512 * 128 * 512
+FLOPS = 2 * (2 * D * Q * I) + 2 * I * Q * E
 
 F32 = mybir.dt.float32
 BF16 = mybir.dt.bfloat16
@@ -20,6 +20,18 @@ AX = mybir.AxisListType
 P = 128
 PACK = 4
 LAST = P - 1
+SLOT_TILES = I // P
+QUADRANT = 32
+WORDS = I // 2
+
+SHARE_REGION = "pool_a"
+KEY_REGION = "pool_b"
+QUERY_REGION = "pool_c"
+VALUE_REGION = "pool_d"
+SCALE_REGION = "pool_e"
+PRODUCT_BANKS = "acc"
+TURN_BANKS = "vturn"
+SHARE_BANK = "turn"
 
 
 def tile_attend_slotmixture_kernel(tc, query, query2, keys_words, keys_scales, share, size, vals, offs, out):
@@ -31,20 +43,23 @@ def tile_attend_slotmixture_kernel(tc, query, query2, keys_words, keys_scales, s
         offsets = sb.tile([P, I // 16], U16, name="offsets")
         nc.sync.dma_start(offsets[:], offs)
 
-        scale_pool = sb.tile([P, T // 4], I32, name="scale_pool", tag="pool_e", align_bytes=64)
+        scale_pool = sb.tile([P, T // 4], I32, name="scale_pool", tag=SCALE_REGION, align_bytes=64)
         nc.vector.memset(scale_pool[:], 0)
-        for quad in range(4):
-            nc.scalar.dma_start(scale_pool[32 * quad : 32 * quad + 4, :], keys_scales[0, 4 * quad : 4 * quad + 4, :].bitcast(I32))
+        for quad in range(P // QUADRANT):
+            nc.scalar.dma_start(
+                scale_pool[QUADRANT * quad : QUADRANT * quad + 4, :],
+                keys_scales[0, 4 * quad : 4 * quad + 4, :].bitcast(I32),
+            )
         size_pad = sb.tile([P, P], F32, name="size_pad")
-        nc.vector.memset(size_pad[0 : P - 4, :], 0.0)
-        nc.scalar.dma_start(size_pad[P - 4 : P, :], size.rearrange("o (j p) -> (o j) p", p=P))
-        share_pool = sb.tile([P, T], F32, name="share_pool", tag="pool_a", align_bytes=64)
+        nc.vector.memset(size_pad[0 : P - SLOT_TILES, :], 0.0)
+        nc.scalar.dma_start(size_pad[P - SLOT_TILES : P, :], size.rearrange("o (j p) -> (o j) p", p=P))
+        share_pool = sb.tile([P, T], F32, name="share_pool", tag=SHARE_REGION, align_bytes=64)
         nc.sync.dma_start(share_pool[LAST:P, :], share[0:1, :])
         nc.vector.memset(share_pool[0:LAST, :], 0.0)
-        q_raw = sb.tile([P, 2, PACK, Q], F32, name="q_raw", tag="pool_c", align_bytes=64)
+        q_raw = sb.tile([P, 2, PACK, Q], F32, name="q_raw", tag=QUERY_REGION, align_bytes=64)
         for n, src in enumerate((query, query2)):
             nc.sync.dma_start(q_raw[:, n], src.rearrange("(p j) w -> p j w", j=PACK))
-        key_pool = sb.tile([P, T], I32, name="key_pool", tag="pool_b", align_bytes=64)
+        key_pool = sb.tile([P, T], I32, name="key_pool", tag=KEY_REGION, align_bytes=64)
         nc.sync.dma_start(key_pool[:], keys_words[0].rearrange("p n t -> p (n t)").bitcast(I32))
 
         val_pool = []
@@ -54,43 +69,41 @@ def tile_attend_slotmixture_kernel(tc, query, query2, keys_words, keys_scales, s
             nc.sync.dma_start(rows[:], vals[c * P : (c + 1) * P, :])
             val_pool.append(rows)
 
-        load_values(0, "pool_d")
+        load_values(0, VALUE_REGION)
         ident = sb.tile([P, P], F32, name="ident")
         make_identity(nc, ident[:])
-        warm = sb.tile([P, 8], F32, name="warm")
-        nc.scalar.activation(warm[0:64, 0:1], size_pad[0:64, 0:1], ACT.Exp)
 
         share_g = sb.tile([P, I], F32, name="share_g", align_bytes=64)
         nc.vector.tensor_copy(share_g[:], share_pool[:].indirect(offsets[:]))
-        load_values(1, "pool_a")
+        load_values(1, SHARE_REGION)
         key_scales = sb.tile([P, I], U8, name="key_scales", align_bytes=64)
         nc.vector.tensor_copy(key_scales[:], scale_pool[:].bitcast(U8).indirect(offsets[:]))
-        key_words = sb.tile([P, I], U32, name="key_words", tag="pool_e", align_bytes=64)
+        key_words = sb.tile([P, I], U32, name="key_words", tag=SCALE_REGION, align_bytes=64)
         nc.vector.tensor_copy(key_words[:], key_pool[:].bitcast(U32).indirect(offsets[:]))
 
-        share_t = ps.tile([P, 4, P], F32, name="share_t", tag="turn")
-        for j in range(4):
+        share_t = ps.tile([P, SLOT_TILES, P], F32, name="share_t", tag=SHARE_BANK)
+        for j in range(SLOT_TILES):
             nc.tensor.transpose(share_t[:, j, :], share_g[:, j * P : (j + 1) * P], ident[:])
         mix = sb.tile([P, 2, 8], F32, name="mix")
-        nc.scalar.copy(mix[:, 0, 0:4], share_t[:, :, LAST])
-        nc.scalar.activation(mix[:, 1, 0:4], share_t[:, :, LAST], ACT.Identity, bias=1.0, scale=-1.0)
+        nc.scalar.copy(mix[:, 0, 0:SLOT_TILES], share_t[:, :, LAST])
+        nc.scalar.activation(mix[:, 1, 0:SLOT_TILES], share_t[:, :, LAST], ACT.Identity, bias=1.0, scale=-1.0)
 
         size_t = ps.tile([P, P], F32, name="size_t")
         nc.tensor.transpose(size_t[:], size_pad[:], ident[:])
-        size_cols = sb.tile([P, 4], F32, name="size_cols")
-        nc.scalar.copy(size_cols[:], size_t[:, P - 4 : P])
+        size_cols = sb.tile([P, SLOT_TILES], F32, name="size_cols")
+        nc.scalar.copy(size_cols[:], size_t[:, P - SLOT_TILES : P])
 
         q_grouped = sb.tile([P, 2, Q, PACK], BF16, name="q_grouped", align_bytes=64)
         for n in range(2):
             nc.scalar.copy(q_grouped[:, n], q_raw[:, n].rearrange("p j w -> p w j"))
-        load_values(2, "pool_c")
+        load_values(2, QUERY_REGION)
         q_codes = sb.tile([P, 2 * Q], U32, name="q_codes", align_bytes=64)
         q_scales = sb.tile([P, 2 * Q], U8, name="q_scales", align_bytes=64)
         nc.vector.quantize_mx(q_codes[:].bitcast(FP8X4), q_scales[:], q_grouped[:].rearrange("p n w j -> p (n w j)"))
 
         parts = []
-        for h in range(2):
-            bank = ps.tile([P, 2, 2, Q], F32, name="score%d" % h, tag="acc", bufs=2)
+        for h in range(SLOT_TILES // 2):
+            bank = ps.tile([P, 2, 2, Q], F32, name="score%d" % h, tag=PRODUCT_BANKS, bufs=2)
             for jj in range(2):
                 j = 2 * h + jj
                 cols = slice(j * P, (j + 1) * P)
@@ -110,29 +123,31 @@ def tile_attend_slotmixture_kernel(tc, query, query2, keys_words, keys_scales, s
                     nc.scalar.activation(part[:, n, :], bank[:, jj, n, :], ACT.Copy, scale=mix[:, n, j : j + 1])
                 parts.append(part)
         mixed = ps.tile([P, I], F32, name="mixed")
-        for j in range(4):
+        for j in range(SLOT_TILES):
             for n in range(2):
-                nc.tensor.matmul(mixed[:, j * P : (j + 1) * P], parts[j][:, n, :], ident[:], start=(n == 0), stop=(n == 1), is_transpose=True)
+                nc.tensor.matmul(
+                    mixed[:, j * P : (j + 1) * P], parts[j][:, n, :], ident[:], start=(n == 0), stop=(n == 1), is_transpose=True
+                )
 
-        size_rows = ps.tile([P, PACK, P], F32, name="size_rows", tag="acc", bufs=2)
-        for t in range(PACK):
-            nc.tensor.transpose(size_rows[:, t, :], size_cols[:, t : t + 1].to_broadcast([P, P]), ident[:])
+        size_rows = ps.tile([P, SLOT_TILES, P], F32, name="size_rows", tag=PRODUCT_BANKS, bufs=2)
+        for j in range(SLOT_TILES):
+            nc.tensor.transpose(size_rows[:, j, :], size_cols[:, j : j + 1].to_broadcast([P, P]), ident[:])
 
-        def gather_values(c):
-            g = sb.tile([P, I], BF16, name="val_g%d" % c, tag="pool_b" if c == 0 else "val_g%d" % c, align_bytes=64)
-            nc.vector.tensor_copy(g[:], val_pool[c][:].indirect(offsets[:]))
-            return g
+        def gather_values(c, tag):
+            gathered = sb.tile([P, I], BF16, name="val_g%d" % c, tag=tag, align_bytes=64)
+            nc.vector.tensor_copy(gathered[:], val_pool[c][:].indirect(offsets[:]))
+            return gathered
 
-        g0 = gather_values(0)
-        load_values(3, "pool_d")
-        g1 = gather_values(1)
-        neg_max = sb.tile([P, 1], F32, name="neg_max", tag="pool_a", align_bytes=64)
+        g0 = gather_values(0, KEY_REGION)
+        load_values(3, VALUE_REGION)
+        g1 = gather_values(1, "val_g1")
+        neg_max = sb.tile([P, 1], F32, name="neg_max", tag=SHARE_REGION, align_bytes=64)
         nc.vector.tensor_reduce(neg_max[:], mixed[:], AX.X, ALU.max, negate=True)
         probs = sb.tile([P, I], F32, name="probs")
         total = sb.tile([P, 1], F32, name="total")
         nc.scalar.activation(probs[:], mixed[:], ACT.Exp, bias=neg_max[:], scale=1.0, accum_out=total[:])
-        g2 = gather_values(2)
-        inv_total = sb.tile([P, 1], F32, name="inv_total", tag="pool_c", align_bytes=64)
+        g2 = gather_values(2, "val_g2")
+        inv_total = sb.tile([P, 1], F32, name="inv_total", tag=QUERY_REGION, align_bytes=64)
         nc.vector.reciprocal(inv_total[:], total[:])
         weights = sb.tile([P, I], BF16, name="weights", align_bytes=64)
         nc.vector.scalar_tensor_tensor(
@@ -144,16 +159,16 @@ def tile_attend_slotmixture_kernel(tc, query, query2, keys_words, keys_scales, s
             ALU.mult,
         )
 
-        def turn(name, tiles, grouped, tag):
+        def turn(name, tiles, dest, tag):
             turned = ps.tile([P, len(tiles), 2, P], F32, name=name, tag=tag, bufs=2)
             for a, tile in enumerate(tiles):
                 words = tile[:].bitcast(F32)
                 for u in range(2):
-                    nc.tensor.transpose(turned[:, a, u, :], words[:, u : I // 2 : 2], ident[:])
-            nc.scalar.copy(grouped.rearrange("p (a x u) -> p a x u", x=P, u=2), turned[:].rearrange("p a u x -> p a x u"))
+                    nc.tensor.transpose(turned[:, a, u, :], words[:, u:WORDS:2], ident[:])
+            nc.scalar.copy(dest.rearrange("p (a x u) -> p a x u", x=P, u=2), turned[:].rearrange("p a u x -> p a x u"))
 
-        def multiply(first, count, v_codes, v_scales):
-            acc = ps.tile([P, count * P], F32, name="acc%d" % first, tag="acc", bufs=2)
+        def multiply(name, v_codes, v_scales, tag, bufs):
+            acc = ps.tile([P, v_scales.shape[1]], F32, name=name, tag=tag, bufs=bufs)
             nc.tensor.matmul_mx(
                 acc[:],
                 lhsT=codes[:, 0:P].bitcast(FP8X4),
@@ -165,15 +180,15 @@ def tile_attend_slotmixture_kernel(tc, query, query2, keys_words, keys_scales, s
             )
             return acc
 
-        g3 = gather_values(3)
-        grouped = sb.tile([P, 8 * P], F32, name="grouped", align_bytes=64)
-        turn("turned01", [g0, g1], grouped[:, 2 * P : 6 * P], "acc")
-        turn("turned2", [g2], grouped[:, 6 * P : 8 * P], "vturn")
-        turn("turnedw", [weights], grouped[:, 0 : 2 * P], "vturn")
-        last_grouped = sb.tile([P, 2 * P], F32, name="last_grouped", align_bytes=64)
-        turn("turned3", [g3], last_grouped[:], "vturn")
+        g3 = gather_values(3, "val_g3")
+        grouped = sb.tile([P, 4 * WORDS], F32, name="grouped", align_bytes=64)
+        turn("turned01", [g0, g1], grouped[:, WORDS : 3 * WORDS], PRODUCT_BANKS)
+        turn("turned2", [g2], grouped[:, 3 * WORDS : 4 * WORDS], TURN_BANKS)
+        turn("turnedw", [weights], grouped[:, 0:WORDS], TURN_BANKS)
+        last_grouped = sb.tile([P, WORDS], F32, name="last_grouped", align_bytes=64)
+        turn("turned3", [g3], last_grouped[:], TURN_BANKS)
 
-        codes = sb.tile([P, 4 * P], U32, name="codes", tag="pool_d", align_bytes=64)
+        codes = sb.tile([P, 4 * P], U32, name="codes", tag=VALUE_REGION, align_bytes=64)
         scales = sb.tile([P, 4 * P], U8, name="scales", align_bytes=64)
         nc.vector.quantize_mx(codes[:].bitcast(FP8X4), scales[:], grouped[:].bitcast(BF16))
         last_codes = sb.tile([P, P], U32, name="last_codes", align_bytes=64)
@@ -181,21 +196,12 @@ def tile_attend_slotmixture_kernel(tc, query, query2, keys_words, keys_scales, s
         nc.vector.quantize_mx(last_codes[:].bitcast(FP8X4), last_scales[:], last_grouped[:].bitcast(BF16))
 
         result = sb.tile([P, 3 * P], F32, name="result")
-        acc = multiply(0, 2, codes[:, P : 3 * P], scales[:, P : 3 * P])
+        acc = multiply("acc0", codes[:, P : 3 * P], scales[:, P : 3 * P], PRODUCT_BANKS, 2)
         nc.scalar.copy(result[:, 0 : 2 * P], acc[:])
-        acc = multiply(2, 1, codes[:, 3 * P : 4 * P], scales[:, 3 * P : 4 * P])
+        acc = multiply("acc2", codes[:, 3 * P : 4 * P], scales[:, 3 * P : 4 * P], PRODUCT_BANKS, 2)
         nc.scalar.copy(result[:, 2 * P : 3 * P], acc[:])
         nc.sync.dma_start(out[:, 0 : 3 * P], result[:])
-        last_acc = ps.tile([P, P], F32, name="last_acc", tag="turn")
-        nc.tensor.matmul_mx(
-            last_acc[:],
-            lhsT=codes[:, 0:P].bitcast(FP8X4),
-            lhsT_scale=scales[:, 0:P],
-            rhs=last_codes[:].bitcast(FP8X4),
-            rhs_scale=last_scales[:],
-            start=True,
-            stop=True,
-        )
+        acc = multiply("last_acc", last_codes[:], last_scales[:], SHARE_BANK, 1)
         last_result = sb.tile([P, P], F32, name="last_result")
-        nc.vector.tensor_copy(last_result[:], last_acc[:])
-        nc.scalar.dma_start(out[:, 3 * P : 4 * P], last_result[:])
+        nc.vector.tensor_copy(last_result[:], acc[:])
+        nc.scalar.dma_start(out[:, 3 * P : E], last_result[:])

from contextlib import ExitStack

import concourse.mybir as mybir
from concourse.masks import make_identity

D, T, I, Q, E = 512, 2048, 512, 128, 512
FLOPS = 2 * (2 * D * Q * I) + 2 * I * Q * E

F32 = mybir.dt.float32
BF16 = mybir.dt.bfloat16
I32 = mybir.dt.int32
U32 = mybir.dt.uint32
U16 = mybir.dt.uint16
U8 = mybir.dt.uint8
FP8X4 = mybir.dt.float8_e4m3fn_x4
ALU = mybir.AluOpType
ACT = mybir.ActivationFunctionType
AX = mybir.AxisListType

P = 128
PACK = 4
LAST = P - 1
SLOT_TILES = I // P
QUADRANT = 32
WORDS = I // 2

SHARE_REGION = "pool_a"
KEY_REGION = "pool_b"
QUERY_REGION = "pool_c"
VALUE_REGION = "pool_d"
SCALE_REGION = "pool_e"
PRODUCT_BANKS = "acc"
TURN_BANKS = "vturn"
SHARE_BANK = "turn"


def tile_attend_slotmixture_kernel(tc, query, query2, keys_words, keys_scales, share, size, vals, offs, out):
    nc = tc.nc
    with ExitStack() as ctx:
        sb = ctx.enter_context(tc.tile_pool(name="sb", bufs=1))
        ps = ctx.enter_context(tc.psum_pool(name="ps", bufs=1))

        offsets = sb.tile([P, I // 16], U16, name="offsets")
        nc.sync.dma_start(offsets[:], offs)

        scale_pool = sb.tile([P, T // 4], I32, name="scale_pool", tag=SCALE_REGION, align_bytes=64)
        nc.vector.memset(scale_pool[:], 0)
        for quad in range(P // QUADRANT):
            nc.scalar.dma_start(
                scale_pool[QUADRANT * quad : QUADRANT * quad + 4, :],
                keys_scales[0, 4 * quad : 4 * quad + 4, :].bitcast(I32),
            )
        size_pad = sb.tile([P, P], F32, name="size_pad")
        nc.vector.memset(size_pad[0 : P - SLOT_TILES, :], 0.0)
        nc.scalar.dma_start(size_pad[P - SLOT_TILES : P, :], size.rearrange("o (j p) -> (o j) p", p=P))
        share_pool = sb.tile([P, T], F32, name="share_pool", tag=SHARE_REGION, align_bytes=64)
        nc.sync.dma_start(share_pool[LAST:P, :], share[0:1, :])
        nc.vector.memset(share_pool[0:LAST, :], 0.0)
        q_raw = sb.tile([P, 2, PACK, Q], F32, name="q_raw", tag=QUERY_REGION, align_bytes=64)
        for n, src in enumerate((query, query2)):
            nc.sync.dma_start(q_raw[:, n], src.rearrange("(p j) w -> p j w", j=PACK))
        key_pool = sb.tile([P, T], I32, name="key_pool", tag=KEY_REGION, align_bytes=64)
        nc.sync.dma_start(key_pool[:], keys_words[0].rearrange("p n t -> p (n t)").bitcast(I32))

        val_pool = []

        def load_values(c, tag):
            rows = sb.tile([P, T], F32, name="val_pool%d" % c, tag=tag, align_bytes=64)
            nc.sync.dma_start(rows[:], vals[c * P : (c + 1) * P, :])
            val_pool.append(rows)

        load_values(0, VALUE_REGION)
        ident = sb.tile([P, P], F32, name="ident")
        make_identity(nc, ident[:])

        share_g = sb.tile([P, I], F32, name="share_g", align_bytes=64)
        nc.vector.tensor_copy(share_g[:], share_pool[:].indirect(offsets[:]))
        load_values(1, SHARE_REGION)
        key_scales = sb.tile([P, I], U8, name="key_scales", align_bytes=64)
        nc.vector.tensor_copy(key_scales[:], scale_pool[:].bitcast(U8).indirect(offsets[:]))
        key_words = sb.tile([P, I], U32, name="key_words", tag=SCALE_REGION, align_bytes=64)
        nc.vector.tensor_copy(key_words[:], key_pool[:].bitcast(U32).indirect(offsets[:]))

        share_t = ps.tile([P, SLOT_TILES, P], F32, name="share_t", tag=SHARE_BANK)
        for j in range(SLOT_TILES):
            nc.tensor.transpose(share_t[:, j, :], share_g[:, j * P : (j + 1) * P], ident[:])
        mix = sb.tile([P, 2, 8], F32, name="mix")
        nc.scalar.copy(mix[:, 0, 0:SLOT_TILES], share_t[:, :, LAST])
        nc.scalar.activation(mix[:, 1, 0:SLOT_TILES], share_t[:, :, LAST], ACT.Identity, bias=1.0, scale=-1.0)

        size_t = ps.tile([P, P], F32, name="size_t")
        nc.tensor.transpose(size_t[:], size_pad[:], ident[:])
        size_cols = sb.tile([P, SLOT_TILES], F32, name="size_cols")
        nc.scalar.copy(size_cols[:], size_t[:, P - SLOT_TILES : P])

        q_grouped = sb.tile([P, 2, Q, PACK], BF16, name="q_grouped", align_bytes=64)
        for n in range(2):
            nc.scalar.copy(q_grouped[:, n], q_raw[:, n].rearrange("p j w -> p w j"))
        load_values(2, QUERY_REGION)
        q_codes = sb.tile([P, 2 * Q], U32, name="q_codes", align_bytes=64)
        q_scales = sb.tile([P, 2 * Q], U8, name="q_scales", align_bytes=64)
        nc.vector.quantize_mx(q_codes[:].bitcast(FP8X4), q_scales[:], q_grouped[:].rearrange("p n w j -> p (n w j)"))

        parts = []
        for h in range(SLOT_TILES // 2):
            bank = ps.tile([P, 2, 2, Q], F32, name="score%d" % h, tag=PRODUCT_BANKS, bufs=2)
            for jj in range(2):
                j = 2 * h + jj
                cols = slice(j * P, (j + 1) * P)
                nc.tensor.matmul_mx(
                    bank[:, jj].rearrange("p n q -> p (n q)"),
                    lhsT=key_words[:, cols].bitcast(FP8X4),
                    lhsT_scale=key_scales[:, cols],
                    rhs=q_codes[:].bitcast(FP8X4),
                    rhs_scale=q_scales[:],
                    start=True,
                    stop=True,
                )
            for jj in range(2):
                j = 2 * h + jj
                part = sb.tile([P, 2, Q], F32, name="part%d" % j)
                for n in range(2):
                    nc.scalar.activation(part[:, n, :], bank[:, jj, n, :], ACT.Copy, scale=mix[:, n, j : j + 1])
                parts.append(part)
        mixed = ps.tile([P, I], F32, name="mixed")
        for j in range(SLOT_TILES):
            for n in range(2):
                nc.tensor.matmul(
                    mixed[:, j * P : (j + 1) * P], parts[j][:, n, :], ident[:], start=(n == 0), stop=(n == 1), is_transpose=True
                )

        size_rows = ps.tile([P, SLOT_TILES, P], F32, name="size_rows", tag=PRODUCT_BANKS, bufs=2)
        for j in range(SLOT_TILES):
            nc.tensor.transpose(size_rows[:, j, :], size_cols[:, j : j + 1].to_broadcast([P, P]), ident[:])

        def gather_values(c, tag):
            gathered = sb.tile([P, I], BF16, name="val_g%d" % c, tag=tag, align_bytes=64)
            nc.vector.tensor_copy(gathered[:], val_pool[c][:].indirect(offsets[:]))
            return gathered

        g0 = gather_values(0, KEY_REGION)
        load_values(3, VALUE_REGION)
        g1 = gather_values(1, "val_g1")
        neg_max = sb.tile([P, 1], F32, name="neg_max", tag=SHARE_REGION, align_bytes=64)
        nc.vector.tensor_reduce(neg_max[:], mixed[:], AX.X, ALU.max, negate=True)
        probs = sb.tile([P, I], F32, name="probs")
        total = sb.tile([P, 1], F32, name="total")
        nc.scalar.activation(probs[:], mixed[:], ACT.Exp, bias=neg_max[:], scale=1.0, accum_out=total[:])
        g2 = gather_values(2, "val_g2")
        inv_total = sb.tile([P, 1], F32, name="inv_total", tag=QUERY_REGION, align_bytes=64)
        nc.vector.reciprocal(inv_total[:], total[:])
        weights = sb.tile([P, I], BF16, name="weights", align_bytes=64)
        nc.vector.scalar_tensor_tensor(
            weights[:],
            probs[:],
            inv_total[:],
            size_rows[:].rearrange("q j p -> q (j p)"),
            ALU.mult,
            ALU.mult,
        )

        def turn(name, tiles, dest, tag):
            turned = ps.tile([P, len(tiles), 2, P], F32, name=name, tag=tag, bufs=2)
            for a, tile in enumerate(tiles):
                words = tile[:].bitcast(F32)
                for u in range(2):
                    nc.tensor.transpose(turned[:, a, u, :], words[:, u:WORDS:2], ident[:])
            nc.scalar.copy(dest.rearrange("p (a x u) -> p a x u", x=P, u=2), turned[:].rearrange("p a u x -> p a x u"))

        def multiply(name, v_codes, v_scales, tag, bufs):
            acc = ps.tile([P, v_scales.shape[1]], F32, name=name, tag=tag, bufs=bufs)
            nc.tensor.matmul_mx(
                acc[:],
                lhsT=codes[:, 0:P].bitcast(FP8X4),
                lhsT_scale=scales[:, 0:P],
                rhs=v_codes.bitcast(FP8X4),
                rhs_scale=v_scales,
                start=True,
                stop=True,
            )
            return acc

        g3 = gather_values(3, "val_g3")
        grouped = sb.tile([P, 4 * WORDS], F32, name="grouped", align_bytes=64)
        turn("turned01", [g0, g1], grouped[:, WORDS : 3 * WORDS], PRODUCT_BANKS)
        turn("turned2", [g2], grouped[:, 3 * WORDS : 4 * WORDS], TURN_BANKS)
        turn("turnedw", [weights], grouped[:, 0:WORDS], TURN_BANKS)
        last_grouped = sb.tile([P, WORDS], F32, name="last_grouped", align_bytes=64)
        turn("turned3", [g3], last_grouped[:], TURN_BANKS)

        codes = sb.tile([P, 4 * P], U32, name="codes", tag=VALUE_REGION, align_bytes=64)
        scales = sb.tile([P, 4 * P], U8, name="scales", align_bytes=64)
        nc.vector.quantize_mx(codes[:].bitcast(FP8X4), scales[:], grouped[:].bitcast(BF16))
        last_codes = sb.tile([P, P], U32, name="last_codes", align_bytes=64)
        last_scales = sb.tile([P, P], U8, name="last_scales", align_bytes=64)
        nc.vector.quantize_mx(last_codes[:].bitcast(FP8X4), last_scales[:], last_grouped[:].bitcast(BF16))

        result = sb.tile([P, 3 * P], F32, name="result")
        acc = multiply("acc0", codes[:, P : 3 * P], scales[:, P : 3 * P], PRODUCT_BANKS, 2)
        nc.scalar.copy(result[:, 0 : 2 * P], acc[:])
        acc = multiply("acc2", codes[:, 3 * P : 4 * P], scales[:, 3 * P : 4 * P], PRODUCT_BANKS, 2)
        nc.scalar.copy(result[:, 2 * P : 3 * P], acc[:])
        nc.sync.dma_start(out[:, 0 : 3 * P], result[:])
        acc = multiply("last_acc", last_codes[:], last_scales[:], SHARE_BANK, 1)
        last_result = sb.tile([P, P], F32, name="last_result")
        nc.vector.tensor_copy(last_result[:], acc[:])
        nc.scalar.dma_start(out[:, 3 * P : E], last_result[:])
